import numpy as np
import ml_dtypes


def mxq(x, axis, fmt="e4m3"):
    dtype, down = {"e4m3": (ml_dtypes.float8_e4m3fn, 7), "e5m2": (ml_dtypes.float8_e5m2, 14)}[fmt]
    v = np.moveaxis(np.asarray(x, np.float32).astype(ml_dtypes.bfloat16).astype(np.float64), axis, -1)
    blocks = v.reshape(v.shape[:-1] + (-1, 32))
    amax = np.abs(blocks).max(-1, keepdims=True)
    byte = np.maximum(np.where(amax > 0, np.frexp(amax)[1] - 1 + 127, 0) - down, 1)
    scale = np.exp2(byte - 127.0)
    codes = (blocks / scale).astype(np.float32).astype(dtype).astype(np.float64)
    return np.moveaxis((codes * scale).reshape(v.shape), -1, axis)


WIDE = False


def mx_kscale(k):
    if not WIDE:
        return np.ones(k)
    levels = np.array([10, -10, 5, -5, 0])
    if k % 512:
        return np.exp2(np.random.permutation(np.resize(levels, k // 32))).repeat(32)
    a = np.empty((k // 512, 16))
    for p in range(k // 512):
        a[p, :8] = np.random.permutation(np.resize(levels, 8))
        for g in range(8):
            far = levels[np.abs(levels - a[p, g]) >= 10]
            a[p, g + 8] = far[np.random.randint(len(far))]
    return np.exp2(a.ravel()).repeat(32)


def f64(x):
    return np.asarray(x).astype(np.float64)


def striped(idx):
    return np.tile(idx.reshape(-1, 16).T, (8, 1)).astype(np.uint16)


def unstriped(offs):
    return offs[:16].T.reshape(-1).astype(np.int64)


def striped8(idx):
    return np.concatenate([x.reshape(-1, 16).T for x in idx]).astype(np.uint16)


def runs(offs, k):
    lists = np.stack([offs[16 * r : 16 * r + 16].T.reshape(-1) for r in range(8)]).astype(np.int64)
    return lists[np.arange(k) % 512 // 64]


def pack_weight(w):
    k, n = w.shape
    w = f64(np.asarray(w, np.float32).astype(ml_dtypes.bfloat16)).reshape(k // 32, 32, n)
    amax = np.abs(w).max(1)
    byte = np.clip(np.where(amax > 0, np.frexp(amax)[1] - 1 + 127 - 7, 1), 1, 254)
    scaled = (w * np.exp2(127.0 - byte)[:, None, :]).reshape(k, n).astype(np.float32)
    words = np.ascontiguousarray(scaled.reshape(k // 512, 128, 4, n).transpose(0, 1, 3, 2)).astype(ml_dtypes.float8_e4m3fn).view(np.uint8)
    return words, np.ascontiguousarray(byte.astype(np.uint8).reshape(k // 512, 16, n))


def unpack_weight(words, scales):
    g, p, n, _ = words.shape
    vals = np.ascontiguousarray(words).view(ml_dtypes.float8_e4m3fn).astype(np.float64) * np.repeat(np.exp2(scales.astype(np.float64) - 127.0), 8, axis=1)[..., None]
    return vals.transpose(0, 1, 3, 2).reshape(g * 512, n)


E2M1 = np.array([0.0, 0.5, 1.0, 1.5, 2.0, 3.0, 4.0, 6.0, -0.0, -0.5, -1.0, -1.5, -2.0, -3.0, -4.0, -6.0])


def pack_fp4(w):
    k, n = w.shape
    w = f64(np.asarray(w, np.float32).astype(ml_dtypes.bfloat16)).reshape(k // 32, 32, n)
    amax = np.abs(w).max(1)
    mant, ex = np.frexp(amax / 6.0)
    byte = np.clip(np.where(amax > 0, np.where(mant > 0.5, ex, ex - 1) + 127, 1), 1, 254)
    scaled = (w * np.exp2(127.0 - byte)[:, None, :]).reshape(k, n).astype(np.float32)
    c = np.ascontiguousarray(scaled.reshape(k // 512, 128, 4, n).transpose(0, 1, 3, 2)).astype(ml_dtypes.float4_e2m1fn).view(np.uint8) & 0xF
    words = (c[..., 0::2] | (c[..., 1::2] << 4)).reshape(k // 512, 128, 2 * n)
    return np.ascontiguousarray(words), np.ascontiguousarray(byte.astype(np.uint8).reshape(k // 512, 16, n))


def unpack_fp4(words, scales):
    g, _, n = scales.shape
    words = np.ascontiguousarray(words).reshape(g, 128, n, 2)
    nib = np.empty((g, 128, n, 4), np.uint8)
    nib[..., 0::2] = words & 0xF
    nib[..., 1::2] = words >> 4
    vals = E2M1[nib] * np.repeat(np.exp2(scales.astype(np.float64) - 127.0), 8, axis=1)[..., None]
    return vals.transpose(0, 1, 3, 2).reshape(g * 512, n)


def planes(y):
    n, m = y.shape
    v = y.astype(np.float32).astype(ml_dtypes.bfloat16).astype(np.float64).reshape(n // 32, 32, m)
    top = np.abs(v).max(1)
    byte = np.clip(np.where(top > 0, np.frexp(top)[1] - 1 + 127 - 7, 1), 1, 254)
    codes = (v * np.exp2(127.0 - byte)[:, None, :]).reshape(n, m).astype(np.float32).astype(ml_dtypes.float8_e4m3fn).view(np.uint8)
    words = codes.reshape(n // 512, 128, 4, m).transpose(0, 1, 3, 2)
    return np.ascontiguousarray(words), np.ascontiguousarray(byte.astype(np.uint8).reshape(n // 512, 16, m))


K, T, S, H, C = 512, 2048, 512, 512, 512


def setup_inputs():
    n = np.random.standard_normal
    s = mx_kscale(K)[:, None]
    packed_xT = pack_weight(n((K, T)) * s)
    packed_w1 = pack_fp4(n((K, H)) / np.sqrt(K) / s)
    return {
        "x_words": packed_xT[0],
        "x_scales": packed_xT[1],
        "w1_words": packed_w1[0],
        "w1_scales": packed_w1[1],
        "gs": (np.random.uniform(0.5, 1.5, (K, 1)) / s).astype(np.float32),
        "offs": striped(np.random.permutation(T)[:S]),
        "q0": striped8(np.stack([np.random.permutation(S) for _ in range(8)])),
        "q1": striped8(np.stack([np.random.permutation(S) for _ in range(8)])),
        "q2": striped8(np.stack([np.random.permutation(S) for _ in range(8)])),
        "q3": striped8(np.stack([np.random.permutation(S) for _ in range(8)])),
        "cand": striped(np.random.permutation(T)[:C]),
    }


def reference(x_words, x_scales, w1_words, w1_scales, gs, offs, q0, q1, q2, q3, cand):
    x_cand = unpack_weight(x_words, x_scales)[:, unstriped(cand)]
    xq = unpack_weight(x_words, x_scales)[:, unstriped(offs)]
    y = unpack_fp4(w1_words, w1_scales).T @ xq
    a = y[np.arange(H)[:, None], runs(q0, H)]
    c = y[np.arange(H)[:, None], runs(q2, H)]
    b = y[np.arange(H)[:, None], runs(q1, H)]
    d = y[np.arange(H)[:, None], runs(q3, H)]
    z = f64(gs) * (((a - c) * (b - d)) / ((a - d) ** 2 + (b - c) ** 2 + 0.5))
    out_0 = 0.0625 * ((x_cand.T @ mxq(z, 0, "e4m3")))
    return (out_0,) + planes(out_0)

@@ -1,0 +1,259 @@
+from contextlib import ExitStack
+
+import concourse.mybir as mybir
+from concourse.masks import make_identity
+
+K, T, S, H, C = 512, 2048, 512, 512, 512
+FLOPS = 2 * K * H * S + 2 * K * C * S
+
+F32 = mybir.dt.float32
+BF16 = mybir.dt.bfloat16
+I32 = mybir.dt.int32
+U32 = mybir.dt.uint32
+U16 = mybir.dt.uint16
+U8 = mybir.dt.uint8
+FP8X4 = mybir.dt.float8_e4m3fn_x4
+FP4X4 = mybir.dt.float4_e2m1fn_x4
+ALU = mybir.AluOpType
+ACT = mybir.ActivationFunctionType
+
+P = 128
+PACK = 4
+HALF = 256
+PIECE = 128
+
+
+def tile_picked_crossrat_none_po_kernel(
+    tc, x_words, x_scales, w1_words, w1_scales, gs, offs, q0, q1, q2, q3, cand, out_0, out_1, out_2
+):
+    nc = tc.nc
+    with ExitStack() as ctx:
+        keep = ctx.enter_context(tc.tile_pool(name="keep", bufs=1))
+        ring = ctx.enter_context(tc.tile_pool(name="ring", bufs=2))
+        psum = ctx.enter_context(tc.psum_pool(name="psum", bufs=1))
+
+        def bank(n):
+            return psum.tile([P, 512], F32, name="bank%d" % n)
+
+        def load_list(src, name):
+            tile = keep.tile([P, 32], U16, name=name)
+            nc.sync.dma_start(tile[:], src)
+            return tile
+
+        def load_scale_rows(tile, src):
+            for quad in range(4):
+                nc.sync.dma_start(
+                    tile[32 * quad : 32 * quad + 4, :].bitcast(I32),
+                    src[0, 4 * quad : 4 * quad + 4, :].bitcast(I32),
+                )
+
+        xs = keep.tile([P, T], U8, name="xs", align_bytes=64)
+        ws = keep.tile([P, H], U8, name="ws", align_bytes=64)
+        nc.vector.memset(xs[:].bitcast(I32), 0)
+        nc.vector.memset(ws[:].bitcast(I32), 0)
+
+        warm_in = keep.tile([P, 1], F32, name="warm_in")
+        warm_out = keep.tile([P, 1], F32, name="warm_out")
+        nc.gpsimd.memset(warm_in[:], 1.0)
+        nc.scalar.activation(warm_out[:], warm_in[:], ACT.Abs_reciprocal_sqrt)
+
+        load_scale_rows(xs, x_scales)
+        offs_t = load_list(offs, "offs_t")
+        cand_t = load_list(cand, "cand_t")
+        ww = keep.tile([P, 2 * H], U8, name="ww", align_bytes=64)
+        nc.sync.dma_start(ww[:].bitcast(I32), w1_words[0].bitcast(I32))
+        xw = keep.tile([P, T], U32, name="xw", align_bytes=64)
+        nc.sync.dma_start(xw[:].bitcast(I32), x_words[0].rearrange("p n t -> p (n t)").bitcast(I32))
+        load_scale_rows(ws, w1_scales)
+        q3_t = load_list(q3, "q3_t")
+        q0_t = load_list(q0, "q0_t")
+        q1_t = load_list(q1, "q1_t")
+        q2_t = load_list(q2, "q2_t")
+        gs_t = keep.tile([P, PACK], F32, name="gs_t")
+        nc.sync.dma_start(gs_t[:], gs.rearrange("(p t) o -> p (t o)", t=PACK))
+
+        ident = keep.tile([P, P], F32, name="ident")
+        make_identity(nc, ident[:])
+
+        xq_s = keep.tile([P, S], U8, name="xq_s", align_bytes=64)
+        nc.vector.tensor_copy(xq_s[:], xs[:].indirect(offs_t[:]))
+        wd = keep.tile([P, 2 * H], U8, name="wd", align_bytes=64)
+        nc.vector.tensor_copy(
+            wd[:].rearrange("p (t m b) -> p t m b", t=PACK, b=2),
+            ww[:].rearrange("p (m t b) -> p t m b", t=PACK, b=2),
+        )
+        xc_g = keep.tile([P, C], U8, name="xc_g", align_bytes=64)
+        nc.vector.tensor_copy(xc_g[:], xs[:].indirect(cand_t[:]))
+        wsd = keep.tile([P, H], U8, name="wsd", align_bytes=64)
+        nc.vector.tensor_copy(
+            wsd[:].rearrange("p (t m) -> p t m", t=PACK),
+            ws[:].rearrange("p (m t) -> p t m", t=PACK),
+        )
+        xq_w = keep.tile([P, S], U32, name="xq_w", align_bytes=64)
+        nc.vector.tensor_copy(xq_w[:], xw[:].indirect(offs_t[:]))
+
+        y_pos, y_neg = [], []
+        for t in range(PACK):
+            acc = bank(t)
+            nc.tensor.matmul_mx(
+                out=acc[:],
+                lhsT=wd[:, 2 * P * t : 2 * P * (t + 1)].bitcast(FP4X4),
+                lhsT_scale=wsd[:, P * t : P * (t + 1)],
+                rhs=xq_w[:].bitcast(FP8X4),
+                rhs_scale=xq_s[:],
+                start=True,
+                stop=True,
+            )
+            pos = keep.tile([P, S], F32, name="y_pos%d" % t)
+            neg = keep.tile([P, S], F32, name="y_neg%d" % t)
+            nc.scalar.copy(pos[:], acc[:])
+            nc.scalar.activation(neg[:], acc[:], ACT.Copy, scale=-1.0)
+            y_pos.append(pos)
+            y_neg.append(neg)
+
+        xc_w = keep.tile([P, C], U32, name="xc_w", align_bytes=64)
+        nc.vector.tensor_copy(xc_w[:].rearrange("p (t m) -> p m t", t=PACK), xw[:].indirect(cand_t[:]))
+        xc_s = keep.tile([P, C], U8, name="xc_s", align_bytes=64)
+        nc.vector.tensor_copy(
+            xc_s[:].rearrange("p (t m) -> p t m", t=PACK),
+            xc_g[:].rearrange("p (m t) -> p t m", t=PACK),
+        )
+
+        units = [(h, pair) for h in range(2) for pair in range(2)]
+        u_t, w_t, s_t = {}, {}, {}
+        rec = [keep.tile([P, PACK, HALF], F32, name="rec%d" % h) for h in range(2)]
+        num = [keep.tile([P, PACK, HALF], F32, name="num%d" % h) for h in range(2)]
+
+        def gathers(n):
+            h, pair = units[n]
+            cols = slice(16 * h, 16 * (h + 1))
+            d = keep.tile([P, 2 * HALF], F32, name="d%d" % n)
+            u = keep.tile([P, 2 * HALF], F32, name="u%d" % n)
+            w = keep.tile([P, 2 * HALF], F32, name="w%d" % n)
+            s = keep.tile([P, 2 * HALF], F32, name="s%d" % n)
+            parts = [(2 * pair + i, slice(HALF * i, HALF * (i + 1))) for i in range(2)]
+            for t, part in parts:
+                nc.vector.tensor_copy(d[:, part], y_pos[t][:].indirect(q3_t[:, cols]))
+            for t, part in parts:
+                nc.vector.tensor_tensor(u[:, part], y_pos[t][:].indirect(q0_t[:, cols]), d[:, part], ALU.subtract)
+            for t, part in parts:
+                nc.vector.tensor_tensor(w[:, part], y_pos[t][:].indirect(q1_t[:, cols]), d[:, part], ALU.subtract)
+            for t, part in parts:
+                nc.vector.tensor_tensor(s[:, part], y_neg[t][:].indirect(q2_t[:, cols]), d[:, part], ALU.add)
+            u_t[n], w_t[n], s_t[n] = u, w, s
+
+        def turned_sum(acc, terms):
+            for b in range(4):
+                blk = slice(P * b, P * (b + 1))
+                for i, term in enumerate(terms):
+                    nc.tensor.matmul(
+                        acc[:, blk], lhsT=term[:, blk], rhs=ident[:],
+                        is_transpose=True, start=(i == 0), stop=(i == len(terms) - 1),
+                    )
+
+        def denominator(n):
+            h, pair = units[n]
+            u_turned = bank(4 + n % 2)
+            turned_sum(u_turned, [u_t[n]])
+            u_sq = ring.tile([P, 2 * HALF], F32, name="u_sq")
+            nc.scalar.activation(u_sq[:], u_turned[:], ACT.Square)
+            q_turned = bank(6 + n % 2)
+            turned_sum(q_turned, [w_t[n], s_t[n]])
+            q_sq = ring.tile([P, 2 * HALF], F32, name="q_sq")
+            nc.scalar.activation(q_sq[:], q_turned[:], ACT.Square)
+            den = bank(n % 2)
+            turned_sum(den, [u_sq, q_sq])
+            root = ring.tile([P, 2 * HALF], F32, name="root")
+            nc.scalar.activation(root[:], den[:], ACT.Abs_reciprocal_sqrt, bias=0.5)
+            nc.scalar.activation(
+                rec[h][:, 2 * pair : 2 * pair + 2, :].rearrange("p t j -> p (t j)"), root[:], ACT.Square
+            )
+
+        def numerator(n):
+            h, pair = units[n]
+            diff = keep.tile([P, 2 * HALF], F32, name="diff%d" % n)
+            nc.vector.tensor_tensor(diff[:], u_t[n][:], s_t[n][:], ALU.add)
+            for i in range(2):
+                t = 2 * pair + i
+                part = slice(HALF * i, HALF * (i + 1))
+                nc.vector.scalar_tensor_tensor(
+                    num[h][:, t, :], diff[:, part], gs_t[:, t : t + 1], w_t[n][:, part], ALU.mult, ALU.mult
+                )
+
+        out_rows = out_0.rearrange("(p t) j -> p t j", t=PACK)
+        out_words = out_1[0].rearrange("p n t -> p (n t)").bitcast(I32)
+        o_s = keep.tile([P, S], U8, name="o_s", align_bytes=64)
+
+        z_b, o_b = {}, {}
+
+        def make_z(m):
+            h, j0 = m // 2, PIECE * (m % 2)
+            zb = keep.tile([P, PACK * PIECE], BF16, name="zb%d" % m, align_bytes=64)
+            nc.vector.tensor_tensor(
+                zb[:].rearrange("p (c i t) -> p c t i", i=4, t=PACK),
+                num[h][:, :, j0 : j0 + PIECE].rearrange("p t (c i) -> p c t i", i=4),
+                rec[h][:, :, j0 : j0 + PIECE].rearrange("p t (c i) -> p c t i", i=4),
+                ALU.mult,
+            )
+            z_b[m] = zb
+
+        def score(m):
+            z_w = keep.tile([P, PIECE], U32, name="z_w%d" % m, align_bytes=64)
+            z_s = keep.tile([P, PIECE], U8, name="z_s%d" % m, align_bytes=64)
+            nc.vector.quantize_mx(out=z_w[:].bitcast(FP8X4), scales=z_s[:], in_=z_b[m][:])
+            acc = bank(2 + m % 2)
+            for t in range(PACK):
+                nc.tensor.matmul_mx(
+                    out=acc[:, PIECE * t : PIECE * (t + 1)],
+                    lhsT=xc_w[:, P * t : P * (t + 1)].bitcast(FP8X4),
+                    lhsT_scale=xc_s[:, P * t : P * (t + 1)],
+                    rhs=z_w[:].bitcast(FP8X4),
+                    rhs_scale=z_s[:],
+                    start=True,
+                    stop=True,
+                )
+            ob = keep.tile([P, PACK * PIECE], BF16, name="ob%d" % m, align_bytes=64)
+            nc.scalar.activation(
+                ob[:].rearrange("p (j t) -> p j t", t=PACK),
+                acc[:].rearrange("p (t j) -> p j t", t=PACK),
+                ACT.Copy,
+                scale=0.0625,
+            )
+            of = keep.tile([P, PACK * PIECE], F32, name="of%d" % m)
+            nc.scalar.activation(of[:], acc[:], ACT.Copy, scale=0.0625)
+            nc.sync.dma_start(
+                out_rows[:, :, PIECE * m : PIECE * (m + 1)], of[:].rearrange("p (t j) -> p t j", t=PACK)
+            )
+            o_b[m] = ob
+
+        def planes(m):
+            cols = slice(PIECE * m, PIECE * (m + 1))
+            o_w = keep.tile([P, PIECE], U32, name="o_w%d" % m, align_bytes=64)
+            nc.vector.quantize_mx(out=o_w[:].bitcast(FP8X4), scales=o_s[:, cols], in_=o_b[m][:])
+            nc.sync.dma_start(out_words[:, cols], o_w[:].bitcast(I32))
+
+        for n in range(4):
+            gathers(n)
+            denominator(n)
+        numerator(0)
+        numerator(1)
+        make_z(0)
+        make_z(1)
+        score(0)
+        numerator(2)
+        score(1)
+        numerator(3)
+        planes(0)
+        make_z(2)
+        planes(1)
+        make_z(3)
+        score(2)
+        score(3)
+        planes(2)
+        planes(3)
+        for quad in range(4):
+            queue = nc.scalar if quad % 2 else nc.sync
+            queue.dma_start(
+                out_2[0, 4 * quad : 4 * quad + 4, :].bitcast(I32),
+                o_s[32 * quad : 32 * quad + 4, :].bitcast(I32),
+            )

@@ -40,9 +40,9 @@ def tile_picked_crossrat_none_po_kernel(
             nc.sync.dma_start(tile[:], src)
             return tile
 
-        def load_scale_rows(tile, src):
+        def load_scale_rows(tile, src, queues):
             for quad in range(4):
-                nc.sync.dma_start(
+                queues[quad % len(queues)].dma_start(
                     tile[32 * quad : 32 * quad + 4, :].bitcast(I32),
                     src[0, 4 * quad : 4 * quad + 4, :].bitcast(I32),
                 )
@@ -54,17 +54,19 @@ def tile_picked_crossrat_none_po_kernel(
 
         warm_in = keep.tile([P, 1], F32, name="warm_in")
         warm_out = keep.tile([P, 1], F32, name="warm_out")
-        nc.gpsimd.memset(warm_in[:], 1.0)
-        nc.scalar.activation(warm_out[:], warm_in[:], ACT.Abs_reciprocal_sqrt)
+        nc.vector.memset(warm_in[:], 1.0)
 
-        load_scale_rows(xs, x_scales)
         offs_t = load_list(offs, "offs_t")
-        cand_t = load_list(cand, "cand_t")
+        xw = keep.tile([P, T], U32, name="xw", align_bytes=64)
+        x_rows = x_words[0].rearrange("p n t -> p (n t)").bitcast(I32)
+        nc.sync.dma_start(xw[:, : T // 2].bitcast(I32), x_rows[:, : T // 2])
+        load_scale_rows(xs, x_scales, [nc.sync, nc.scalar])
+        nc.scalar.activation(warm_out[:], warm_in[:], ACT.Abs_reciprocal_sqrt)
+        nc.sync.dma_start(xw[:, T // 2 :].bitcast(I32), x_rows[:, T // 2 :])
         ww = keep.tile([P, 2 * H], U8, name="ww", align_bytes=64)
         nc.sync.dma_start(ww[:].bitcast(I32), w1_words[0].bitcast(I32))
-        xw = keep.tile([P, T], U32, name="xw", align_bytes=64)
-        nc.sync.dma_start(xw[:].bitcast(I32), x_words[0].rearrange("p n t -> p (n t)").bitcast(I32))
-        load_scale_rows(ws, w1_scales)
+        load_scale_rows(ws, w1_scales, [nc.sync])
+        cand_t = load_list(cand, "cand_t")
         q3_t = load_list(q3, "q3_t")
         q0_t = load_list(q0, "q0_t")
         q1_t = load_list(q1, "q1_t")
@@ -78,21 +80,19 @@ def tile_picked_crossrat_none_po_kernel(
         xq_s = keep.tile([P, S], U8, name="xq_s", align_bytes=64)
         nc.vector.tensor_copy(xq_s[:], xs[:].indirect(offs_t[:]))
         wd = keep.tile([P, 2 * H], U8, name="wd", align_bytes=64)
-        nc.vector.tensor_copy(
+        nc.gpsimd.tensor_copy(
             wd[:].rearrange("p (t m b) -> p t m b", t=PACK, b=2),
             ww[:].rearrange("p (m t b) -> p t m b", t=PACK, b=2),
         )
-        xc_g = keep.tile([P, C], U8, name="xc_g", align_bytes=64)
-        nc.vector.tensor_copy(xc_g[:], xs[:].indirect(cand_t[:]))
         wsd = keep.tile([P, H], U8, name="wsd", align_bytes=64)
-        nc.vector.tensor_copy(
+        nc.gpsimd.tensor_copy(
             wsd[:].rearrange("p (t m) -> p t m", t=PACK),
             ws[:].rearrange("p (m t) -> p t m", t=PACK),
         )
         xq_w = keep.tile([P, S], U32, name="xq_w", align_bytes=64)
         nc.vector.tensor_copy(xq_w[:], xw[:].indirect(offs_t[:]))
 
-        y_pos, y_neg = [], []
+        y_pos, y_neg, y_acc = [], [], []
         for t in range(PACK):
             acc = bank(t)
             nc.tensor.matmul_mx(
@@ -104,13 +104,17 @@ def tile_picked_crossrat_none_po_kernel(
                 start=True,
                 stop=True,
             )
-            pos = keep.tile([P, S], F32, name="y_pos%d" % t)
-            neg = keep.tile([P, S], F32, name="y_neg%d" % t)
-            nc.scalar.copy(pos[:], acc[:])
-            nc.scalar.activation(neg[:], acc[:], ACT.Copy, scale=-1.0)
-            y_pos.append(pos)
-            y_neg.append(neg)
+            y_acc.append(acc)
+            y_pos.append(keep.tile([P, S], F32, name="y_pos%d" % t))
+            y_neg.append(keep.tile([P, S], F32, name="y_neg%d" % t))
+        for pair in range(2):
+            for t in (2 * pair, 2 * pair + 1):
+                nc.scalar.copy(y_pos[t][:], y_acc[t][:])
+            for t in (2 * pair, 2 * pair + 1):
+                nc.scalar.activation(y_neg[t][:], y_acc[t][:], ACT.Copy, scale=-1.0)
 
+        xc_g = keep.tile([P, C], U8, name="xc_g", align_bytes=64)
+        nc.vector.tensor_copy(xc_g[:], xs[:].indirect(cand_t[:]))
         xc_w = keep.tile([P, C], U32, name="xc_w", align_bytes=64)
         nc.vector.tensor_copy(xc_w[:].rearrange("p (t m) -> p m t", t=PACK), xw[:].indirect(cand_t[:]))
         xc_s = keep.tile([P, C], U8, name="xc_s", align_bytes=64)
@@ -119,31 +123,31 @@ def tile_picked_crossrat_none_po_kernel(
             xc_g[:].rearrange("p (m t) -> p t m", t=PACK),
         )
 
-        units = [(h, pair) for h in range(2) for pair in range(2)]
-        u_t, w_t, s_t = {}, {}, {}
+        u_t, w_t, s_t, p_t = {}, {}, {}, {}
         rec = [keep.tile([P, PACK, HALF], F32, name="rec%d" % h) for h in range(2)]
-        num = [keep.tile([P, PACK, HALF], F32, name="num%d" % h) for h in range(2)]
+        num = {}
 
-        def gathers(n):
-            h, pair = units[n]
+        def gathers(h, pair, d_tag, by_tile):
             cols = slice(16 * h, 16 * (h + 1))
-            d = keep.tile([P, 2 * HALF], F32, name="d%d" % n)
+            n = 2 * h + pair
+            d = keep.tile([P, 2 * HALF], F32, name="d%d" % n, tag=d_tag)
             u = keep.tile([P, 2 * HALF], F32, name="u%d" % n)
             w = keep.tile([P, 2 * HALF], F32, name="w%d" % n)
             s = keep.tile([P, 2 * HALF], F32, name="s%d" % n)
             parts = [(2 * pair + i, slice(HALF * i, HALF * (i + 1))) for i in range(2)]
             for t, part in parts:
                 nc.vector.tensor_copy(d[:, part], y_pos[t][:].indirect(q3_t[:, cols]))
-            for t, part in parts:
-                nc.vector.tensor_tensor(u[:, part], y_pos[t][:].indirect(q0_t[:, cols]), d[:, part], ALU.subtract)
-            for t, part in parts:
-                nc.vector.tensor_tensor(w[:, part], y_pos[t][:].indirect(q1_t[:, cols]), d[:, part], ALU.subtract)
-            for t, part in parts:
-                nc.vector.tensor_tensor(s[:, part], y_neg[t][:].indirect(q2_t[:, cols]), d[:, part], ALU.add)
+            fused = [(u, y_pos, q0_t, ALU.subtract), (w, y_pos, q1_t, ALU.subtract), (s, y_neg, q2_t, ALU.add)]
+            if by_tile:
+                order = [(f, tp) for tp in parts for f in fused]
+            else:
+                order = [(f, tp) for f in fused for tp in parts]
+            for (dst, windows, places, op), (t, part) in order:
+                nc.vector.tensor_tensor(dst[:, part], windows[t][:].indirect(places[:, cols]), d[:, part], op)
             u_t[n], w_t[n], s_t[n] = u, w, s
 
-        def turned_sum(acc, terms):
-            for b in range(4):
+        def turned_sum(acc, terms, width):
+            for b in range(width // P):
                 blk = slice(P * b, P * (b + 1))
                 for i, term in enumerate(terms):
                     nc.tensor.matmul(
@@ -151,106 +155,139 @@ def tile_picked_crossrat_none_po_kernel(
                         is_transpose=True, start=(i == 0), stop=(i == len(terms) - 1),
                     )
 
-        def denominator(n):
-            h, pair = units[n]
-            u_turned = bank(4 + n % 2)
-            turned_sum(u_turned, [u_t[n]])
-            u_sq = ring.tile([P, 2 * HALF], F32, name="u_sq")
-            nc.scalar.activation(u_sq[:], u_turned[:], ACT.Square)
-            q_turned = bank(6 + n % 2)
-            turned_sum(q_turned, [w_t[n], s_t[n]])
-            q_sq = ring.tile([P, 2 * HALF], F32, name="q_sq")
-            nc.scalar.activation(q_sq[:], q_turned[:], ACT.Square)
-            den = bank(n % 2)
-            turned_sum(den, [u_sq, q_sq])
-            root = ring.tile([P, 2 * HALF], F32, name="root")
-            nc.scalar.activation(root[:], den[:], ACT.Abs_reciprocal_sqrt, bias=0.5)
+        def denominator(h, pair, i0, count, den_bank, p_bank, u_bank=0, q_bank=1):
+            n = 2 * h + pair
+            width = count * HALF
+            part = slice(i0 * HALF, i0 * HALF + width)
+            u, w, s = u_t[n][:, part], w_t[n][:, part], s_t[n][:, part]
+            u_turned = bank(u_bank)
+            turned_sum(u_turned, [u], width)
+            u_sq = ring.tile([P, 512], F32, name="u_sq")
+            nc.scalar.activation(u_sq[:, :width], u_turned[:, :width], ACT.Square)
+            q_turned = bank(q_bank)
+            turned_sum(q_turned, [w, s], width)
+            q_sq = ring.tile([P, 512], F32, name="q_sq")
+            nc.scalar.activation(q_sq[:, :width], q_turned[:, :width], ACT.Square)
+            if p_bank is not None:
+                p_turned = bank(2)
+                turned_sum(p_turned, [u, s], width)
+                p_sb = ring.tile([P, 512], F32, name="p_sb")
+                nc.scalar.copy(p_sb[:], p_turned[:])
+            root = ring.tile([P, 512], F32, name="root")
+            share = width // len(den_bank)
+            for k, which in enumerate(den_bank):
+                den = bank(which)
+                run = slice(share * k, share * (k + 1))
+                turned_sum(den, [u_sq[:, run], q_sq[:, run]], share)
+                nc.scalar.activation(root[:, run], den[:, :share], ACT.Abs_reciprocal_sqrt, bias=0.5)
+            if p_bank is not None:
+                p_t[n] = bank(p_bank)
+                turned_sum(p_t[n], [p_sb], width)
+            t0 = 2 * pair + i0
             nc.scalar.activation(
-                rec[h][:, 2 * pair : 2 * pair + 2, :].rearrange("p t j -> p (t j)"), root[:], ACT.Square
+                rec[h][:, t0 : t0 + count, :].rearrange("p t j -> p (t j)"), root[:, :width], ACT.Square
             )
 
-        def numerator(n):
-            h, pair = units[n]
-            diff = keep.tile([P, 2 * HALF], F32, name="diff%d" % n)
-            nc.vector.tensor_tensor(diff[:], u_t[n][:], s_t[n][:], ALU.add)
+        def numerator(h, pair):
+            n = 2 * h + pair
+            if h not in num:
+                num[h] = keep.tile([P, PACK, HALF], F32, name="num%d" % h, tag="num%d" % h)
+            if n not in p_t:
+                p_t[n] = keep.tile([P, 2 * HALF], F32, name="diff%d" % n, tag="num0")
+                nc.vector.tensor_tensor(p_t[n][:], u_t[n][:], s_t[n][:], ALU.add)
             for i in range(2):
                 t = 2 * pair + i
                 part = slice(HALF * i, HALF * (i + 1))
                 nc.vector.scalar_tensor_tensor(
-                    num[h][:, t, :], diff[:, part], gs_t[:, t : t + 1], w_t[n][:, part], ALU.mult, ALU.mult
+                    num[h][:, t, :], p_t[n][:, part], gs_t[:, t : t + 1], w_t[n][:, part], ALU.mult, ALU.mult
                 )
 
         out_rows = out_0.rearrange("(p t) j -> p t j", t=PACK)
         out_words = out_1[0].rearrange("p n t -> p (n t)").bitcast(I32)
         o_s = keep.tile([P, S], U8, name="o_s", align_bytes=64)
+        last = S // PIECE - 1
 
-        z_b, o_b = {}, {}
+        z_b, z_q, o_b = {}, {}, {}
 
-        def make_z(m):
-            h, j0 = m // 2, PIECE * (m % 2)
-            zb = keep.tile([P, PACK * PIECE], BF16, name="zb%d" % m, align_bytes=64)
+        def make_z(m, count):
+            h, j0, wide = m // 2, PIECE * (m % 2), PIECE * count
+            zb = keep.tile([P, PACK * wide], BF16, name="zb%d" % m, align_bytes=64)
             nc.vector.tensor_tensor(
                 zb[:].rearrange("p (c i t) -> p c t i", i=4, t=PACK),
-                num[h][:, :, j0 : j0 + PIECE].rearrange("p t (c i) -> p c t i", i=4),
-                rec[h][:, :, j0 : j0 + PIECE].rearrange("p t (c i) -> p c t i", i=4),
+                num[h][:, :, j0 : j0 + wide].rearrange("p t (c i) -> p c t i", i=4),
+                rec[h][:, :, j0 : j0 + wide].rearrange("p t (c i) -> p c t i", i=4),
                 ALU.mult,
             )
             z_b[m] = zb
 
-        def score(m):
-            z_w = keep.tile([P, PIECE], U32, name="z_w%d" % m, align_bytes=64)
-            z_s = keep.tile([P, PIECE], U8, name="z_s%d" % m, align_bytes=64)
+        def quantize_z(m, count):
+            z_w = keep.tile([P, PIECE * count], U32, name="z_w%d" % m, align_bytes=64)
+            z_s = keep.tile([P, PIECE * count], U8, name="z_s%d" % m, align_bytes=64)
             nc.vector.quantize_mx(out=z_w[:].bitcast(FP8X4), scales=z_s[:], in_=z_b[m][:])
-            acc = bank(2 + m % 2)
+            ob = keep.tile([P, PIECE * count, PACK], BF16, name="ob%d" % m, align_bytes=64)
+            for k in range(count):
+                cols = slice(PIECE * k, PIECE * (k + 1))
+                z_q[m + k] = (z_w[:, cols], z_s[:, cols], ob[:, cols, :])
+            o_b[m] = ob
+
+        def score(m, out_bank):
+            z_w, z_s, ob = z_q[m]
+            acc = bank(out_bank)
             for t in range(PACK):
                 nc.tensor.matmul_mx(
                     out=acc[:, PIECE * t : PIECE * (t + 1)],
                     lhsT=xc_w[:, P * t : P * (t + 1)].bitcast(FP8X4),
                     lhsT_scale=xc_s[:, P * t : P * (t + 1)],
-                    rhs=z_w[:].bitcast(FP8X4),
-                    rhs_scale=z_s[:],
+                    rhs=z_w.bitcast(FP8X4),
+                    rhs_scale=z_s,
                     start=True,
                     stop=True,
                 )
-            ob = keep.tile([P, PACK * PIECE], BF16, name="ob%d" % m, align_bytes=64)
-            nc.scalar.activation(
-                ob[:].rearrange("p (j t) -> p j t", t=PACK),
-                acc[:].rearrange("p (t j) -> p j t", t=PACK),
-                ACT.Copy,
-                scale=0.0625,
-            )
+            by_column = acc[:].rearrange("p (t j) -> p j t", t=PACK)
+            if m == last:
+                nc.vector.tensor_scalar_mul(ob, by_column, 0.0625)
+            else:
+                nc.scalar.activation(ob, by_column, ACT.Copy, scale=0.0625)
             of = keep.tile([P, PACK * PIECE], F32, name="of%d" % m)
             nc.scalar.activation(of[:], acc[:], ACT.Copy, scale=0.0625)
             nc.sync.dma_start(
                 out_rows[:, :, PIECE * m : PIECE * (m + 1)], of[:].rearrange("p (t j) -> p t j", t=PACK)
             )
-            o_b[m] = ob
 
-        def planes(m):
-            cols = slice(PIECE * m, PIECE * (m + 1))
-            o_w = keep.tile([P, PIECE], U32, name="o_w%d" % m, align_bytes=64)
-            nc.vector.quantize_mx(out=o_w[:].bitcast(FP8X4), scales=o_s[:, cols], in_=o_b[m][:])
+        def planes(m, count):
+            cols = slice(PIECE * m, PIECE * (m + count))
+            o_w = keep.tile([P, PIECE * count], U32, name="o_w%d" % m, align_bytes=64)
+            nc.vector.quantize_mx(
+                out=o_w[:].bitcast(FP8X4), scales=o_s[:, cols], in_=o_b[m][:].rearrange("p j t -> p (j t)")
+            )
             nc.sync.dma_start(out_words[:, cols], o_w[:].bitcast(I32))
 
-        for n in range(4):
-            gathers(n)
-            denominator(n)
-        numerator(0)
-        numerator(1)
-        make_z(0)
-        make_z(1)
-        score(0)
-        numerator(2)
-        score(1)
-        numerator(3)
-        planes(0)
-        make_z(2)
-        planes(1)
-        make_z(3)
-        score(2)
-        score(3)
-        planes(2)
-        planes(3)
+        gathers(0, 0, "d0", False)
+        denominator(0, 0, 0, 2, [3], 5)
+        gathers(0, 1, "d1", False)
+        denominator(0, 1, 0, 2, [4], 6)
+        gathers(1, 0, "d2", False)
+        denominator(1, 0, 0, 2, [3], 7)
+        gathers(1, 1, "d3", True)
+        denominator(1, 1, 0, 1, [4], None)
+        denominator(1, 1, 1, 1, [3, 0], None)
+        numerator(0, 0)
+        numerator(0, 1)
+        make_z(0, 2)
+        quantize_z(0, 2)
+        score(0, 3)
+        score(1, 0)
+        numerator(1, 1)
+        numerator(1, 0)
+        make_z(2, 1)
+        make_z(3, 1)
+        quantize_z(2, 1)
+        score(2, 5)
+        quantize_z(3, 1)
+        score(3, 6)
+        planes(0, 2)
+        planes(2, 1)
+        planes(3, 1)
         for quad in range(4):
             queue = nc.scalar if quad % 2 else nc.sync
             queue.dma_start(

from contextlib import ExitStack

import concourse.mybir as mybir
from concourse.masks import make_identity

K, T, S, H, C = 512, 2048, 512, 512, 512
FLOPS = 2 * K * H * S + 2 * K * C * S

F32 = mybir.dt.float32
BF16 = mybir.dt.bfloat16
I32 = mybir.dt.int32
U32 = mybir.dt.uint32
U16 = mybir.dt.uint16
U8 = mybir.dt.uint8
FP8X4 = mybir.dt.float8_e4m3fn_x4
FP4X4 = mybir.dt.float4_e2m1fn_x4
ALU = mybir.AluOpType
ACT = mybir.ActivationFunctionType

P = 128
PACK = 4
HALF = 256
PIECE = 128


def tile_picked_crossrat_none_po_kernel(
    tc, x_words, x_scales, w1_words, w1_scales, gs, offs, q0, q1, q2, q3, cand, out_0, out_1, out_2
):
    nc = tc.nc
    with ExitStack() as ctx:
        keep = ctx.enter_context(tc.tile_pool(name="keep", bufs=1))
        ring = ctx.enter_context(tc.tile_pool(name="ring", bufs=2))
        psum = ctx.enter_context(tc.psum_pool(name="psum", bufs=1))

        def bank(n):
            return psum.tile([P, 512], F32, name="bank%d" % n)

        def load_list(src, name):
            tile = keep.tile([P, 32], U16, name=name)
            nc.sync.dma_start(tile[:], src)
            return tile

        def load_scale_rows(tile, src, queues):
            for quad in range(4):
                queues[quad % len(queues)].dma_start(
                    tile[32 * quad : 32 * quad + 4, :].bitcast(I32),
                    src[0, 4 * quad : 4 * quad + 4, :].bitcast(I32),
                )

        xs = keep.tile([P, T], U8, name="xs", align_bytes=64)
        ws = keep.tile([P, H], U8, name="ws", align_bytes=64)
        nc.vector.memset(xs[:].bitcast(I32), 0)
        nc.vector.memset(ws[:].bitcast(I32), 0)

        warm_in = keep.tile([P, 1], F32, name="warm_in")
        warm_out = keep.tile([P, 1], F32, name="warm_out")
        nc.vector.memset(warm_in[:], 1.0)

        offs_t = load_list(offs, "offs_t")
        xw = keep.tile([P, T], U32, name="xw", align_bytes=64)
        x_rows = x_words[0].rearrange("p n t -> p (n t)").bitcast(I32)
        nc.sync.dma_start(xw[:, : T // 2].bitcast(I32), x_rows[:, : T // 2])
        load_scale_rows(xs, x_scales, [nc.sync, nc.scalar])
        nc.scalar.activation(warm_out[:], warm_in[:], ACT.Abs_reciprocal_sqrt)
        nc.sync.dma_start(xw[:, T // 2 :].bitcast(I32), x_rows[:, T // 2 :])
        ww = keep.tile([P, 2 * H], U8, name="ww", align_bytes=64)
        nc.sync.dma_start(ww[:].bitcast(I32), w1_words[0].bitcast(I32))
        load_scale_rows(ws, w1_scales, [nc.sync])
        cand_t = load_list(cand, "cand_t")
        q3_t = load_list(q3, "q3_t")
        q0_t = load_list(q0, "q0_t")
        q1_t = load_list(q1, "q1_t")
        q2_t = load_list(q2, "q2_t")
        gs_t = keep.tile([P, PACK], F32, name="gs_t")
        nc.sync.dma_start(gs_t[:], gs.rearrange("(p t) o -> p (t o)", t=PACK))

        ident = keep.tile([P, P], F32, name="ident")
        make_identity(nc, ident[:])

        xq_s = keep.tile([P, S], U8, name="xq_s", align_bytes=64)
        nc.vector.tensor_copy(xq_s[:], xs[:].indirect(offs_t[:]))
        wd = keep.tile([P, 2 * H], U8, name="wd", align_bytes=64)
        nc.gpsimd.tensor_copy(
            wd[:].rearrange("p (t m b) -> p t m b", t=PACK, b=2),
            ww[:].rearrange("p (m t b) -> p t m b", t=PACK, b=2),
        )
        wsd = keep.tile([P, H], U8, name="wsd", align_bytes=64)
        nc.gpsimd.tensor_copy(
            wsd[:].rearrange("p (t m) -> p t m", t=PACK),
            ws[:].rearrange("p (m t) -> p t m", t=PACK),
        )
        xq_w = keep.tile([P, S], U32, name="xq_w", align_bytes=64)
        nc.vector.tensor_copy(xq_w[:], xw[:].indirect(offs_t[:]))

        y_pos, y_neg, y_acc = [], [], []
        for t in range(PACK):
            acc = bank(t)
            nc.tensor.matmul_mx(
                out=acc[:],
                lhsT=wd[:, 2 * P * t : 2 * P * (t + 1)].bitcast(FP4X4),
                lhsT_scale=wsd[:, P * t : P * (t + 1)],
                rhs=xq_w[:].bitcast(FP8X4),
                rhs_scale=xq_s[:],
                start=True,
                stop=True,
            )
            y_acc.append(acc)
            y_pos.append(keep.tile([P, S], F32, name="y_pos%d" % t))
            y_neg.append(keep.tile([P, S], F32, name="y_neg%d" % t))
        for pair in range(2):
            for t in (2 * pair, 2 * pair + 1):
                nc.scalar.copy(y_pos[t][:], y_acc[t][:])
            for t in (2 * pair, 2 * pair + 1):
                nc.scalar.activation(y_neg[t][:], y_acc[t][:], ACT.Copy, scale=-1.0)

        xc_g = keep.tile([P, C], U8, name="xc_g", align_bytes=64)
        nc.vector.tensor_copy(xc_g[:], xs[:].indirect(cand_t[:]))
        xc_w = keep.tile([P, C], U32, name="xc_w", align_bytes=64)
        nc.vector.tensor_copy(xc_w[:].rearrange("p (t m) -> p m t", t=PACK), xw[:].indirect(cand_t[:]))
        xc_s = keep.tile([P, C], U8, name="xc_s", align_bytes=64)
        nc.vector.tensor_copy(
            xc_s[:].rearrange("p (t m) -> p t m", t=PACK),
            xc_g[:].rearrange("p (m t) -> p t m", t=PACK),
        )

        u_t, w_t, s_t, p_t = {}, {}, {}, {}
        rec = [keep.tile([P, PACK, HALF], F32, name="rec%d" % h) for h in range(2)]
        num = {}

        def gathers(h, pair, d_tag, by_tile):
            cols = slice(16 * h, 16 * (h + 1))
            n = 2 * h + pair
            d = keep.tile([P, 2 * HALF], F32, name="d%d" % n, tag=d_tag)
            u = keep.tile([P, 2 * HALF], F32, name="u%d" % n)
            w = keep.tile([P, 2 * HALF], F32, name="w%d" % n)
            s = keep.tile([P, 2 * HALF], F32, name="s%d" % n)
            parts = [(2 * pair + i, slice(HALF * i, HALF * (i + 1))) for i in range(2)]
            for t, part in parts:
                nc.vector.tensor_copy(d[:, part], y_pos[t][:].indirect(q3_t[:, cols]))
            fused = [(u, y_pos, q0_t, ALU.subtract), (w, y_pos, q1_t, ALU.subtract), (s, y_neg, q2_t, ALU.add)]
            if by_tile:
                order = [(f, tp) for tp in parts for f in fused]
            else:
                order = [(f, tp) for f in fused for tp in parts]
            for (dst, windows, places, op), (t, part) in order:
                nc.vector.tensor_tensor(dst[:, part], windows[t][:].indirect(places[:, cols]), d[:, part], op)
            u_t[n], w_t[n], s_t[n] = u, w, s

        def turned_sum(acc, terms, width):
            for b in range(width // P):
                blk = slice(P * b, P * (b + 1))
                for i, term in enumerate(terms):
                    nc.tensor.matmul(
                        acc[:, blk], lhsT=term[:, blk], rhs=ident[:],
                        is_transpose=True, start=(i == 0), stop=(i == len(terms) - 1),
                    )

        def denominator(h, pair, i0, count, den_bank, p_bank, u_bank=0, q_bank=1):
            n = 2 * h + pair
            width = count * HALF
            part = slice(i0 * HALF, i0 * HALF + width)
            u, w, s = u_t[n][:, part], w_t[n][:, part], s_t[n][:, part]
            u_turned = bank(u_bank)
            turned_sum(u_turned, [u], width)
            u_sq = ring.tile([P, 512], F32, name="u_sq")
            nc.scalar.activation(u_sq[:, :width], u_turned[:, :width], ACT.Square)
            q_turned = bank(q_bank)
            turned_sum(q_turned, [w, s], width)
            q_sq = ring.tile([P, 512], F32, name="q_sq")
            nc.scalar.activation(q_sq[:, :width], q_turned[:, :width], ACT.Square)
            if p_bank is not None:
                p_turned = bank(2)
                turned_sum(p_turned, [u, s], width)
                p_sb = ring.tile([P, 512], F32, name="p_sb")
                nc.scalar.copy(p_sb[:], p_turned[:])
            root = ring.tile([P, 512], F32, name="root")
            share = width // len(den_bank)
            for k, which in enumerate(den_bank):
                den = bank(which)
                run = slice(share * k, share * (k + 1))
                turned_sum(den, [u_sq[:, run], q_sq[:, run]], share)
                nc.scalar.activation(root[:, run], den[:, :share], ACT.Abs_reciprocal_sqrt, bias=0.5)
            if p_bank is not None:
                p_t[n] = bank(p_bank)
                turned_sum(p_t[n], [p_sb], width)
            t0 = 2 * pair + i0
            nc.scalar.activation(
                rec[h][:, t0 : t0 + count, :].rearrange("p t j -> p (t j)"), root[:, :width], ACT.Square
            )

        def numerator(h, pair):
            n = 2 * h + pair
            if h not in num:
                num[h] = keep.tile([P, PACK, HALF], F32, name="num%d" % h, tag="num%d" % h)
            if n not in p_t:
                p_t[n] = keep.tile([P, 2 * HALF], F32, name="diff%d" % n, tag="num0")
                nc.vector.tensor_tensor(p_t[n][:], u_t[n][:], s_t[n][:], ALU.add)
            for i in range(2):
                t = 2 * pair + i
                part = slice(HALF * i, HALF * (i + 1))
                nc.vector.scalar_tensor_tensor(
                    num[h][:, t, :], p_t[n][:, part], gs_t[:, t : t + 1], w_t[n][:, part], ALU.mult, ALU.mult
                )

        out_rows = out_0.rearrange("(p t) j -> p t j", t=PACK)
        out_words = out_1[0].rearrange("p n t -> p (n t)").bitcast(I32)
        o_s = keep.tile([P, S], U8, name="o_s", align_bytes=64)
        last = S // PIECE - 1

        z_b, z_q, o_b = {}, {}, {}

        def make_z(m, count):
            h, j0, wide = m // 2, PIECE * (m % 2), PIECE * count
            zb = keep.tile([P, PACK * wide], BF16, name="zb%d" % m, align_bytes=64)
            nc.vector.tensor_tensor(
                zb[:].rearrange("p (c i t) -> p c t i", i=4, t=PACK),
                num[h][:, :, j0 : j0 + wide].rearrange("p t (c i) -> p c t i", i=4),
                rec[h][:, :, j0 : j0 + wide].rearrange("p t (c i) -> p c t i", i=4),
                ALU.mult,
            )
            z_b[m] = zb

        def quantize_z(m, count):
            z_w = keep.tile([P, PIECE * count], U32, name="z_w%d" % m, align_bytes=64)
            z_s = keep.tile([P, PIECE * count], U8, name="z_s%d" % m, align_bytes=64)
            nc.vector.quantize_mx(out=z_w[:].bitcast(FP8X4), scales=z_s[:], in_=z_b[m][:])
            ob = keep.tile([P, PIECE * count, PACK], BF16, name="ob%d" % m, align_bytes=64)
            for k in range(count):
                cols = slice(PIECE * k, PIECE * (k + 1))
                z_q[m + k] = (z_w[:, cols], z_s[:, cols], ob[:, cols, :])
            o_b[m] = ob

        def score(m, out_bank):
            z_w, z_s, ob = z_q[m]
            acc = bank(out_bank)
            for t in range(PACK):
                nc.tensor.matmul_mx(
                    out=acc[:, PIECE * t : PIECE * (t + 1)],
                    lhsT=xc_w[:, P * t : P * (t + 1)].bitcast(FP8X4),
                    lhsT_scale=xc_s[:, P * t : P * (t + 1)],
                    rhs=z_w.bitcast(FP8X4),
                    rhs_scale=z_s,
                    start=True,
                    stop=True,
                )
            by_column = acc[:].rearrange("p (t j) -> p j t", t=PACK)
            if m == last:
                nc.vector.tensor_scalar_mul(ob, by_column, 0.0625)
            else:
                nc.scalar.activation(ob, by_column, ACT.Copy, scale=0.0625)
            of = keep.tile([P, PACK * PIECE], F32, name="of%d" % m)
            nc.scalar.activation(of[:], acc[:], ACT.Copy, scale=0.0625)
            nc.sync.dma_start(
                out_rows[:, :, PIECE * m : PIECE * (m + 1)], of[:].rearrange("p (t j) -> p t j", t=PACK)
            )

        def planes(m, count):
            cols = slice(PIECE * m, PIECE * (m + count))
            o_w = keep.tile([P, PIECE * count], U32, name="o_w%d" % m, align_bytes=64)
            nc.vector.quantize_mx(
                out=o_w[:].bitcast(FP8X4), scales=o_s[:, cols], in_=o_b[m][:].rearrange("p j t -> p (j t)")
            )
            nc.sync.dma_start(out_words[:, cols], o_w[:].bitcast(I32))

        gathers(0, 0, "d0", False)
        denominator(0, 0, 0, 2, [3], 5)
        gathers(0, 1, "d1", False)
        denominator(0, 1, 0, 2, [4], 6)
        gathers(1, 0, "d2", False)
        denominator(1, 0, 0, 2, [3], 7)
        gathers(1, 1, "d3", True)
        denominator(1, 1, 0, 1, [4], None)
        denominator(1, 1, 1, 1, [3, 0], None)
        numerator(0, 0)
        numerator(0, 1)
        make_z(0, 2)
        quantize_z(0, 2)
        score(0, 3)
        score(1, 0)
        numerator(1, 1)
        numerator(1, 0)
        make_z(2, 1)
        make_z(3, 1)
        quantize_z(2, 1)
        score(2, 5)
        quantize_z(3, 1)
        score(3, 6)
        planes(0, 2)
        planes(2, 1)
        planes(3, 1)
        for quad in range(4):
            queue = nc.scalar if quad % 2 else nc.sync
            queue.dma_start(
                out_2[0, 4 * quad : 4 * quad + 4, :].bitcast(I32),
                o_s[32 * quad : 32 * quad + 4, :].bitcast(I32),
            )
